import numpy as np, ml_dtypes
CORES = [24,48,72,152,176,200]
N = 6
WB, KB, QP = 1, 1, 32
def setup_inputs(rng):
    return {"q": rng.standard_normal((N, 128, QP), dtype=np.float32).astype(ml_dtypes.bfloat16), "k": rng.standard_normal((N, 128, KB * 128), dtype=np.float32).astype(ml_dtypes.bfloat16), "v": rng.standard_normal((N, 128, KB * 128), dtype=np.float32).astype(ml_dtypes.bfloat16)}
def setup_inputs_big(rng):
    d = setup_inputs(rng)
    for k in ("q", "k", "v"): d[k] = (d[k].astype(np.float32) * 1024.0).astype(d[k].dtype)
    return d
def setup_inputs_small(rng):
    d = setup_inputs(rng)
    for k in ("q", "k", "v"): d[k] = (d[k].astype(np.float32) * (1 / 1024.0)).astype(d[k].dtype)
    return d
def setup_inputs_apart(rng):
    d = setup_inputs(rng)
    f = (10.0 ** rng.permutation(np.linspace(-1.5, 1.5, N))).astype(np.float32).reshape(N, 1, 1)
    for k in ("q", "k", "v"): d[k] = (d[k].astype(np.float32) * f).astype(d[k].dtype)
    return d
def reference(q, k, v):
    Q, K, V = q.astype(np.float64), k.astype(np.float64), v.astype(np.float64)
    y = np.zeros((N, 128, QP))
    for r in range(N):
        for j in range(max(0, r - WB), r + 1):
            for b in range(KB):
                S = np.maximum(K[j][:, 128 * b:128 * b + 128].T @ Q[r], 0.0)
                y[r] += V[j][:, 128 * b:128 * b + 128].T @ S
    return {"y": y.astype(ml_dtypes.bfloat16 if q.dtype != np.float64 else np.float64)}

from concourse.bass import DstId, RemoteDMATransfer
from concourse.mybir import AluOpType

SCRATCH = {
    "kst": ("dram", [128, 128], "bfloat16"),
    "vst": ("dram", [128, 128], "bfloat16"),
    "ksb": ("sbuf", [128, 128], "bfloat16"),
    "vsb": ("sbuf", [128, 128], "bfloat16"),
    "qsb": ("sbuf", [128, 32], "bfloat16"),
    "kpv": ("sbuf", [128, 128], "bfloat16"),
    "vpv": ("sbuf", [128, 128], "bfloat16"),
    "zero": ("sbuf", [128, 32], "float32"),
    "s0": ("sbuf", [128, 32], "bfloat16"),
    "s1": ("sbuf", [128, 32], "bfloat16"),
    "ysb": ("sbuf", [128, 32], "bfloat16"),
    "p0": ("psum", [128, 512], "float32"),
    "p1": ("psum", [128, 512], "float32"),
    "po": ("psum", [128, 512], "float32"),
}
SEMAPHORES = ["staged", "ldkq", "ldv", "land", "sent", "karr", "varr",
              "zs", "m0", "r0", "m1", "r1", "m2", "cp", "stored"]

HAND = 4


def _engines(mask):
    return [1 << b for b in range(mask.bit_length()) if (mask >> b) & 1]


def _split(mask, parts, each):
    e = _engines(mask)
    e = e[::len(e) // (parts * each)][:parts * each]
    return [sum(e[i * each:(i + 1) * each]) for i in range(parts)]


def _carriers(T, topo, r):
    src, dst = T.cores[r], T.cores[r + 1]
    if topo.may_write(src, dst):
        return src, src
    world = range(topo.CORES_PER_HOST * (1 + max(topo.host(c) for c in T.cores)))
    able = [c for c in world
            if topo.host(c) == topo.host(src) and topo.chip(c) == topo.chip(src) and T.rank_of(c) is None
            and topo.may_write(src, c) and topo.may_write(c, dst)]
    near = [c for c in able if topo.die(c) == topo.die(src)]
    far = [c for c in able if topo.die(c) != topo.die(src)]
    return near[0], far[0]


def _direct_masks(topo, src, dst):
    m = topo.mask(src, dst)
    return _split(m, 2, len(_engines(m)) // 2)


def rank_program(g, core, T, topo):
    S = T.sem
    n = len(T.cores)
    rank = T.rank_of(core)

    if rank is None:
        for r in range(n - 1):
            kc, vc = _carriers(T, topo, r)
            dst = T.cores[r + 1]
            for c, piece, out, arr in ((kc, T.kst, T.kpv, S.karr), (vc, T.vst, T.vpv, S.varr)):
                if c != core:
                    continue
                m = topo.mask(core, dst)
                rid, pid = topo.addr(dst, core)
                g.wait_ge(S.land, HAND)
                g.remote_dma(out_ap=out[:], in_ap=piece[:], remote_sem=arr, local_sem=S.sent,
                             pid=pid, routing_id=rid, dma_engine_mask=m)
                g.wait_ge(S.sent, len(_engines(m)))
        return

    sends = rank + 1 < n
    takes = rank > 0

    if sends:
        g.sync.dma_start(T.kst[:], T.k[:]).then_inc(S.staged, 16)
        g.scalar.dma_start(T.vst[:], T.v[:]).then_inc(S.staged, 16)
    g.sync.dma_start(T.qsb[:], T.q[:]).then_inc(S.ldkq, 16)
    g.sync.dma_start(T.ksb[:], T.k[:]).then_inc(S.ldkq, 16)
    g.scalar.dma_start(T.vsb[:], T.v[:]).then_inc(S.ldv, 16)
    g.vector.memset(T.zero[:], 0.0).then_inc(S.zs, 1)

    if sends:
        dst = T.cores[rank + 1]
        kc, vc = _carriers(T, topo, rank)
        if kc == core:
            masks = _direct_masks(topo, core, dst)
            plan = ((dst, T.kst, T.kpv, S.karr, masks[0]), (dst, T.vst, T.vpv, S.varr, masks[1]))
        else:
            masks = _split(topo.mask(core, kc) & topo.mask(core, vc), 2, HAND)
            plan = ((kc, T.kst, T.kst, S.land, masks[0]), (vc, T.vst, T.vst, S.land, masks[1]))
        transfers = []
        for to, src_t, dst_t, sem, m in plan:
            rid, pid = topo.addr(to, core)
            transfers.append(RemoteDMATransfer(dst_ids=[DstId(rid=rid, pnc=pid)], dma_engine_mask=m, remote_sem=sem,
                                               src=src_t[:], dst=dst_t[:]))
        g.wait_ge(S.staged, 32)
        g.remote_dma_fused(transfers, local_sem=S.sent)
        g.wait_ge(S.sent, sum(len(_engines(m)) for m in masks))

    g.tensor.wait_ge(S.ldkq, 32)
    g.tensor.matmul(T.p0[:, 0:32], T.ksb[:], T.qsb[:], True, True).then_inc(S.m0, 1)
    g.vector.wait_ge(S.zs, 1)
    g.vector.wait_ge(S.m0, 1)
    g.vector.tensor_tensor(T.s0[:], T.p0[:, 0:32], T.zero[:], AluOpType.max).then_inc(S.r0, 1)
    g.tensor.wait_ge(S.r0, 1)
    g.tensor.wait_ge(S.ldv, 16)
    own = g.tensor.matmul(T.po[:, 0:32], T.vsb[:], T.s0[:], True, not takes)
    if not takes:
        own.then_inc(S.m2, 1)

    if takes:
        prev = T.cores[rank - 1]
        kc, vc = _carriers(T, topo, rank - 1)
        if kc == prev:
            nk, nv = [len(_engines(m)) for m in _direct_masks(topo, prev, core)]
        else:
            nk, nv = len(_engines(topo.mask(kc, core))), len(_engines(topo.mask(vc, core)))
        g.tensor.wait_ge(S.karr, nk)
        g.tensor.matmul(T.p1[:, 0:32], T.kpv[:], T.qsb[:], True, True).then_inc(S.m1, 1)
        g.vector.wait_ge(S.m1, 1)
        g.vector.tensor_tensor(T.s1[:], T.p1[:, 0:32], T.zero[:], AluOpType.max).then_inc(S.r1, 1)
        g.tensor.wait_ge(S.r1, 1)
        g.tensor.wait_ge(S.varr, nv)
        g.tensor.matmul(T.po[:, 0:32], T.vpv[:], T.s1[:], False, True).then_inc(S.m2, 1)

    g.vector.wait_ge(S.m2, 1)
    g.vector.tensor_copy(T.ysb[:], T.po[:, 0:32]).then_inc(S.cp, 1)
    g.sync.wait_ge(S.cp, 1)
    g.sync.dma_start(T.y[:], T.ysb[:]).then_inc(S.stored, 16)
    g.sync.wait_ge(S.stored, 16)
